import numpy as np
import ml_dtypes


def mxq(x, axis, fmt="e4m3"):
    dtype, down = {"e4m3": (ml_dtypes.float8_e4m3fn, 7), "e5m2": (ml_dtypes.float8_e5m2, 14)}[fmt]
    v = np.moveaxis(np.asarray(x, np.float32).astype(ml_dtypes.bfloat16).astype(np.float64), axis, -1)
    blocks = v.reshape(v.shape[:-1] + (-1, 32))
    amax = np.abs(blocks).max(-1, keepdims=True)
    byte = np.maximum(np.where(amax > 0, np.frexp(amax)[1] - 1 + 127, 0) - down, 1)
    scale = np.exp2(byte - 127.0)
    codes = (blocks / scale).astype(np.float32).astype(dtype).astype(np.float64)
    return np.moveaxis((codes * scale).reshape(v.shape), -1, axis)


WIDE = False


def mx_kscale(k):
    if not WIDE:
        return np.ones(k)
    levels = np.array([10, -10, 5, -5, 0])
    if k % 512:
        return np.exp2(np.random.permutation(np.resize(levels, k // 32))).repeat(32)
    a = np.empty((k // 512, 16))
    for p in range(k // 512):
        a[p, :8] = np.random.permutation(np.resize(levels, 8))
        for g in range(8):
            far = levels[np.abs(levels - a[p, g]) >= 10]
            a[p, g + 8] = far[np.random.randint(len(far))]
    return np.exp2(a.ravel()).repeat(32)


def f64(x):
    return np.asarray(x).astype(np.float64)


def striped(idx):
    return np.tile(idx.reshape(-1, 16).T, (8, 1)).astype(np.uint16)


def unstriped(offs):
    return offs[:16].T.reshape(-1).astype(np.int64)


def striped8(idx):
    return np.concatenate([x.reshape(-1, 16).T for x in idx]).astype(np.uint16)


def runs(offs, k):
    lists = np.stack([offs[16 * r : 16 * r + 16].T.reshape(-1) for r in range(8)]).astype(np.int64)
    return lists[np.arange(k) % 512 // 64]


def pack_weight(w):
    k, n = w.shape
    w = f64(np.asarray(w, np.float32).astype(ml_dtypes.bfloat16)).reshape(k // 32, 32, n)
    amax = np.abs(w).max(1)
    byte = np.clip(np.where(amax > 0, np.frexp(amax)[1] - 1 + 127 - 7, 1), 1, 254)
    scaled = (w * np.exp2(127.0 - byte)[:, None, :]).reshape(k, n).astype(np.float32)
    words = np.ascontiguousarray(scaled.reshape(k // 512, 128, 4, n).transpose(0, 1, 3, 2)).astype(ml_dtypes.float8_e4m3fn).view(np.uint8)
    return words, np.ascontiguousarray(byte.astype(np.uint8).reshape(k // 512, 16, n))


def unpack_weight(words, scales):
    g, p, n, _ = words.shape
    vals = np.ascontiguousarray(words).view(ml_dtypes.float8_e4m3fn).astype(np.float64) * np.repeat(np.exp2(scales.astype(np.float64) - 127.0), 8, axis=1)[..., None]
    return vals.transpose(0, 1, 3, 2).reshape(g * 512, n)

def planes(y):
    n, m = y.shape
    v = y.astype(np.float32).astype(ml_dtypes.bfloat16).astype(np.float64).reshape(n // 32, 32, m)
    top = np.abs(v).max(1)
    byte = np.clip(np.where(top > 0, np.frexp(top)[1] - 1 + 127 - 7, 1), 1, 254)
    codes = (v * np.exp2(127.0 - byte)[:, None, :]).reshape(n, m).astype(np.float32).astype(ml_dtypes.float8_e4m3fn).view(np.uint8)
    words = codes.reshape(n // 512, 128, 4, m).transpose(0, 1, 3, 2)
    return np.ascontiguousarray(words), np.ascontiguousarray(byte.astype(np.uint8).reshape(n // 512, 16, m))


K, T, S, N, H = 512, 2048, 256, 512, 512


def setup_inputs():
    n = np.random.standard_normal
    s = mx_kscale(K)[:, None]
    u = mx_kscale(H)
    packed_xT = pack_weight(n((K, T)) * s)
    packed_w1 = pack_weight(n((K, H)) / np.sqrt(K) / s)
    packed_w2 = pack_weight(n((H, N)) / np.sqrt(2 * H) / u[:, None])
    packed_w3 = pack_weight(n((K, N)) / np.sqrt(2 * K) / s)
    return {
        "x_words": packed_xT[0],
        "x_scales": packed_xT[1],
        "w1_words": packed_w1[0],
        "w1_scales": packed_w1[1],
        "gn": (np.random.uniform(0.5, 1.5, (H, 1)) * u[:, None]).astype(np.float32),
        "w2_words": packed_w2[0],
        "w2_scales": packed_w2[1],
        "w3_words": packed_w3[0],
        "w3_scales": packed_w3[1],
        "tau": np.random.uniform(0.3, 0.9, (N, 1)).astype(np.float32),
        "offs": striped8(np.random.randint(0, T, (8, S))),
        "n1": striped(np.random.permutation(S)),
        "two": striped(np.random.permutation(T)[:S]),
        "n2": striped8(np.stack([np.random.permutation(S) for _ in range(8)])),
        "n3": striped8(np.stack([np.random.permutation(S) for _ in range(8)])),
    }


def reference(x_words, x_scales, w1_words, w1_scales, gn, w2_words, w2_scales, w3_words, w3_scales, tau, offs, n1, two, n2, n3):
    xq = unpack_weight(x_words, x_scales)[np.arange(K)[:, None], runs(offs, K)]
    y = unpack_weight(w1_words, w1_scales).T @ xq
    pa = y[:, unstriped(n1)]
    z = f64(gn) * ((2.0 * (y * pa)) / ((y) ** 2 + (pa) ** 2 + 0.5))
    x_two = unpack_weight(x_words, x_scales)[:, unstriped(two)]
    h = unpack_weight(w2_words, w2_scales).T @ mxq(z, 0, "e4m3") + unpack_weight(w3_words, w3_scales).T @ x_two
    top = h.max(axis=1, keepdims=True)
    ea = np.exp(f64(tau) * (h[np.arange(N)[:, None], runs(n2, N)] - top))
    ea2 = np.exp(f64(tau) * (h[np.arange(N)[:, None], runs(n3, N)] - top))
    out_0 = h + np.log(ea + ea2 + 0.25)
    return (out_0,) + planes(out_0)

@@ -1,0 +1,249 @@
+from contextlib import ExitStack
+
+import concourse.mybir as mybir
+
+K, T, S, N, H = 512, 2048, 256, 512, 512
+FLOPS = 2 * S * (K * H + H * N + K * N)
+
+F32 = mybir.dt.float32
+BF16 = mybir.dt.bfloat16
+I32 = mybir.dt.int32
+U32 = mybir.dt.uint32
+U16 = mybir.dt.uint16
+U8 = mybir.dt.uint8
+FP8X4 = mybir.dt.float8_e4m3fn_x4
+ALU = mybir.AluOpType
+ACT = mybir.ActivationFunctionType
+
+P = 128
+PACK = 4
+QUAD = 32
+Y_WINDOW = S + 8
+H_WINDOW = 2 * S
+HALF = S // 2
+CAST_SPLIT = 192
+
+
+def as_words(packed):
+    return packed[0].rearrange("p n t -> p (n t)").bitcast(I32)
+
+
+def deal(engine_copy, dealt, raw, run):
+    engine_copy(
+        out=dealt.rearrange("p (t c i) -> p c t i", t=PACK, i=run),
+        in_=raw.rearrange("p (c i t) -> p c t i", t=PACK, i=run),
+    )
+
+
+def tile_picked_hmixharmelg_none_po_kernel(
+    tc, x_words, x_scales, w1_words, w1_scales, gn, w2_words, w2_scales, w3_words, w3_scales, tau, offs, n1, two, n2, n3, out_0, out_1, out_2
+):
+    nc = tc.nc
+    with ExitStack() as ctx:
+        keep = ctx.enter_context(tc.tile_pool(name="keep", bufs=1))
+        psum = ctx.enter_context(tc.psum_pool(name="psum", bufs=1))
+
+        lists = {}
+        for name in ("offs", "two", "n1", "n2", "n3"):
+            lists[name] = keep.tile([P, S // 16], U16, name="list_" + name)
+
+        x_table = keep.tile([P, T], U32, align_bytes=64)
+        x_rows = keep.tile([P, T], U8, align_bytes=64, tag="rows_then_w23")
+        w1_raw = keep.tile([P, H], U32, align_bytes=64)
+        w1_rows = keep.tile([P, H], U8, align_bytes=64)
+
+        nc.vector.memset(x_rows[:, : T // 2].bitcast(I32), 0)
+        nc.gpsimd.memset(x_rows[:, T // 2 :].bitcast(I32), 0)
+        nc.vector.memset(w1_rows[:].bitcast(I32), 0)
+        nc.sync.dma_start(lists["offs"][:], offs)
+        nc.sync.dma_start(w1_raw[:].bitcast(I32), as_words(w1_words))
+        for name, source in (("two", two), ("n1", n1), ("n2", n2), ("n3", n3)):
+            nc.sync.dma_start(lists[name][:], source)
+        nc.sync.dma_start(x_rows[0:P:8, :].bitcast(I32), x_scales[0].bitcast(I32))
+        nc.sync.dma_start(x_table[:].bitcast(I32), as_words(x_words))
+        for q in range(4):
+            nc.sync.dma_start(w1_rows[QUAD * q : QUAD * q + 4, :].bitcast(I32), w1_scales[0, 4 * q : 4 * q + 4, :].bitcast(I32))
+
+        gain = keep.tile([P, PACK], F32)
+        rate = keep.tile([P, PACK], F32)
+        nc.gpsimd.dma_start(gain[:], gn.rearrange("(p t) o -> p (t o)", t=PACK))
+        nc.gpsimd.dma_start(rate[:], tau.rearrange("(p t) o -> p (t o)", t=PACK))
+
+        minus_rate = keep.tile([P, PACK], F32)
+        nc.vector.tensor_scalar(minus_rate[:], rate[:], -1.0, None, ALU.mult)
+
+        y_win = [keep.tile([P, Y_WINDOW], F32, name="y_win%d" % t) for t in range(PACK)]
+        h_win = [keep.tile([P, H_WINDOW], F32, name="h_win%d" % t) for t in range(PACK)]
+        for t in range(PACK):
+            nc.gpsimd.memset(y_win[t][:, S:], 0.0)
+        for t in range(PACK):
+            nc.vector.memset(h_win[t][:, S:], 0.0)
+
+        def pick_scales(name, tag):
+            picked = keep.tile([P, S], U8, align_bytes=64, name="picked_" + name, tag=tag)
+            plane = keep.tile([P, S], U8, align_bytes=64, name="plane_" + name)
+            nc.vector.tensor_copy(out=picked[:], in_=x_rows[:].indirect(lists[name][:]))
+            nc.vector.tensor_copy(out=plane[:].bitcast(I32), in_=picked[:].bitcast(I32))
+            return picked, plane
+
+        def place_rows(queue, picked, plane):
+            for r in range(1, 4):
+                queue.dma_start(plane[r:P:QUAD, :].bitcast(I32), picked[8 * r : P : QUAD, :].bitcast(I32))
+
+        w1_codes = keep.tile([P, H], U32, align_bytes=64)
+        deal(nc.scalar.copy, w1_codes[:], w1_raw[:], 4)
+        xq_picked, xq_plane = pick_scales("offs", "picked_then_w23")
+        place_rows(nc.sync, xq_picked, xq_plane)
+        x2_picked, x2_plane = pick_scales("two", "picked_two")
+
+        xq_codes = keep.tile([P, S], U32, align_bytes=64)
+        x2_codes = keep.tile([P, S], U32, align_bytes=64)
+        nc.vector.tensor_copy(out=xq_codes[:], in_=x_table[:].indirect(lists["offs"][:]))
+        nc.vector.tensor_copy(out=x2_codes[:], in_=x_table[:].indirect(lists["two"][:]))
+        w1_plane = keep.tile([P, H], U8, align_bytes=64)
+        for t in range(PACK):
+            nc.gpsimd.tensor_copy(out=w1_plane[:, P * t : P * (t + 1)], in_=w1_rows[:, t:H:PACK])
+
+        w23_raw = keep.tile([P, 2, N], U32, align_bytes=64, tag="rows_then_w23")
+        w23_rows = keep.tile([P, N], U8, align_bytes=64, tag="picked_then_w23")
+        nc.sync.dma_start(w23_raw[:, 0, :].bitcast(I32), as_words(w3_words))
+        nc.sync.dma_start(w23_raw[:, 1, :].bitcast(I32), as_words(w2_words))
+        place_rows(nc.sync, x2_picked, x2_plane)
+        nc.gpsimd.memset(w23_rows[:].bitcast(I32), 0)
+        for k, scales in ((0, w3_scales), (4, w2_scales)):
+            for q in range(4):
+                nc.sync.dma_start(w23_rows[QUAD * q + k : QUAD * q + k + 4, :].bitcast(I32), scales[0, 4 * q : 4 * q + 4, :].bitcast(I32))
+        w3_codes = keep.tile([P, N], U32, align_bytes=64)
+        w2_codes = keep.tile([P, N], U32, align_bytes=64)
+        w23_plane = keep.tile([P, N], U8, align_bytes=64)
+
+        y_bank = [psum.tile([P, S], F32, name="y_bank%d" % t) for t in range(PACK)]
+        h_bank = [psum.tile([P, S], F32, name="h_bank%d" % t) for t in range(PACK)]
+        for t in range(PACK):
+            cols = slice(P * t, P * (t + 1))
+            nc.tensor.matmul_mx(
+                out=y_bank[t][:], lhsT=w1_codes[:, cols].bitcast(FP8X4), lhsT_scale=w1_plane[:, cols],
+                rhs=xq_codes[:].bitcast(FP8X4), rhs_scale=xq_plane[:], start=True, stop=True,
+            )
+
+        partner = keep.tile([P, PACK, S], F32)
+        y_sq = keep.tile([P, PACK, S], F32)
+        p_sq = keep.tile([P, PACK, S], F32)
+        both_sq = keep.tile([P, PACK, S], F32)
+        cross = keep.tile([P, PACK, S], F32)
+        root = keep.tile([P, PACK, S], F32)
+        inverse = keep.tile([P, PACK, S], F32)
+
+        def fetch(t):
+            nc.scalar.activation(partner[:, t, :], y_win[t][:].indirect(lists["n1"][:]), ACT.Copy)
+
+        def square_y(t):
+            nc.vector.tensor_tensor(y_sq[:, t, :], y_bank[t][:], y_win[t][:, :S], ALU.mult)
+
+        def square_partner(t):
+            nc.scalar.activation(p_sq[:, t, :], partner[:, t, :], ACT.Square)
+
+        def add_squares(t):
+            nc.vector.tensor_tensor(both_sq[:, t, :], y_sq[:, t, :], p_sq[:, t, :], ALU.add)
+
+        def numerator(t):
+            nc.vector.scalar_tensor_tensor(cross[:, t, :], y_bank[t][:], gain[:, t : t + 1], partner[:, t, :], ALU.mult, ALU.mult)
+
+        def inverse_root(t):
+            nc.scalar.activation(root[:, t, :], both_sq[:, t, :], ACT.Abs_reciprocal_sqrt, bias=0.25, scale=0.5)
+
+        def square_root_back(t):
+            if t < PACK - 1:
+                nc.vector.tensor_tensor(inverse[:, t, :], root[:, t, :], root[:, t, :], ALU.mult)
+            else:
+                nc.scalar.activation(inverse[:, t, :], root[:, t, :], ACT.Square)
+
+        for t in range(PACK):
+            nc.vector.tensor_copy(out=y_win[t][:, :S], in_=y_bank[t][:])
+        for t in range(PACK):
+            fetch(t)
+            if t > 0:
+                square_partner(t - 1)
+        square_partner(PACK - 1)
+        for t in range(PACK):
+            square_y(t)
+        for t in range(PACK):
+            numerator(t)
+            add_squares(t)
+        for t in range(PACK):
+            inverse_root(t)
+        for t in range(PACK):
+            square_root_back(t)
+
+        deal(nc.gpsimd.tensor_copy, w3_codes[:], w23_raw[:, 0, :], 4)
+        deal(nc.gpsimd.tensor_copy, w2_codes[:], w23_raw[:, 1, :], 4)
+        deal(nc.gpsimd.tensor_copy, w23_plane[:], w23_rows[:], 16)
+        for t in range(PACK):
+            cols = slice(P * t, P * (t + 1))
+            nc.tensor.matmul_mx(
+                out=h_bank[t][:], lhsT=w3_codes[:, cols].bitcast(FP8X4), lhsT_scale=w23_plane[:, cols],
+                rhs=x2_codes[:].bitcast(FP8X4), rhs_scale=x2_plane[:], start=True, stop=False,
+            )
+
+        z_rounded = keep.tile([P, S, PACK], BF16, align_bytes=64)
+        z_codes = keep.tile([P, S], U32, align_bytes=64)
+        z_plane = keep.tile([P, S], U8, align_bytes=64)
+        halves = [slice(0, HALF), slice(HALF, S)]
+        for cols in halves:
+            nc.vector.tensor_tensor(
+                z_rounded[:, cols, :].rearrange("p (c i) t -> p c t i", i=4),
+                cross[:, :, cols].rearrange("p t (c i) -> p c t i", i=4),
+                inverse[:, :, cols].rearrange("p t (c i) -> p c t i", i=4),
+                ALU.mult,
+            )
+        for cols in halves:
+            nc.vector.quantize_mx(
+                out=z_codes[:, cols].bitcast(FP8X4), scales=z_plane[:, cols], in_=z_rounded[:, cols, :].rearrange("p c t -> p (c t)")
+            )
+        for t in range(PACK):
+            cols = slice(P * t, P * (t + 1))
+            for places in halves:
+                nc.tensor.matmul_mx(
+                    out=h_bank[t][:, places], lhsT=w2_codes[:, cols].bitcast(FP8X4), lhsT_scale=w23_plane[4:P, cols],
+                    rhs=z_codes[:, places].bitcast(FP8X4), rhs_scale=z_plane[:, places], start=False, stop=places is halves[-1],
+                )
+
+        top = keep.tile([P, PACK], F32)
+        shift = keep.tile([P, PACK], F32)
+        ea = keep.tile([P, PACK, S], F32)
+        eb = keep.tile([P, PACK, S], F32)
+        total = keep.tile([P, PACK, S], F32)
+        logs = keep.tile([P, PACK, S], F32)
+        result = keep.tile([P, PACK, S], F32)
+        for t in range(PACK):
+            one = slice(t, t + 1)
+            nc.vector.tensor_scalar(h_win[t][:, :S], h_bank[t][:], 1.0, None, ALU.mult, ALU.max, accum_out=top[:, one])
+            if t == 0:
+                nc.scalar.activation(shift[:, one], top[:, one], ACT.Copy, scale=minus_rate[:, one])
+            else:
+                nc.vector.tensor_scalar(shift[:, one], top[:, one], minus_rate[:, one], None, ALU.mult)
+        for t in range(PACK):
+            one = slice(t, t + 1)
+            nc.scalar.activation(ea[:, t, :], h_win[t][:].indirect(lists["n2"][:]), ACT.Exp, bias=shift[:, one], scale=rate[:, one])
+            nc.scalar.activation(eb[:, t, :], h_win[t][:].indirect(lists["n3"][:]), ACT.Exp, bias=shift[:, one], scale=rate[:, one])
+            nc.vector.tensor_tensor(total[:, t, :], ea[:, t, :], eb[:, t, :], ALU.add)
+        out_rows = out_0.rearrange("(p t) c -> p t c", t=PACK)
+        for t in range(PACK):
+            nc.scalar.activation(logs[:, t, :], total[:, t, :], ACT.Ln, bias=0.25)
+            nc.vector.tensor_tensor(result[:, t, :], h_bank[t][:], logs[:, t, :], ALU.add)
+            if t % 2:
+                nc.sync.dma_start(out_rows[:, t - 1 : t + 1, :], result[:, t - 1 : t + 1, :])
+
+        out_rounded = keep.tile([P, S, PACK], BF16, align_bytes=64)
+        out_codes = keep.tile([P, S], U32, align_bytes=64)
+        out_plane = keep.tile([P, S], U8, align_bytes=64)
+        for copy, cols in ((nc.vector.tensor_copy, slice(0, CAST_SPLIT)), (nc.scalar.copy, slice(CAST_SPLIT, S))):
+            copy(
+                out=out_rounded[:, cols, :].rearrange("p (c i) t -> p c t i", i=4),
+                in_=result[:, :, cols].rearrange("p t (c i) -> p c t i", i=4),
+            )
+        nc.vector.quantize_mx(out=out_codes[:].bitcast(FP8X4), scales=out_plane[:], in_=out_rounded[:].rearrange("p c t -> p (c t)"))
+        nc.sync.dma_start(as_words(out_1), out_codes[:].bitcast(I32))
+        for q in range(4):
+            queue = nc.scalar if q % 2 else nc.sync
+            queue.dma_start(out_2[0, 4 * q : 4 * q + 4, :].bitcast(I32), out_plane[QUAD * q : QUAD * q + 4, :].bitcast(I32))

@@ -52,25 +52,28 @@ def tile_picked_hmixharmelg_none_po_kernel(
         w1_raw = keep.tile([P, H], U32, align_bytes=64)
         w1_rows = keep.tile([P, H], U8, align_bytes=64)
 
+        warm_in = keep.tile([P, 1], F32)
+        warm_out = keep.tile([P, 1], F32)
         nc.vector.memset(x_rows[:, : T // 2].bitcast(I32), 0)
         nc.gpsimd.memset(x_rows[:, T // 2 :].bitcast(I32), 0)
         nc.vector.memset(w1_rows[:].bitcast(I32), 0)
+        nc.gpsimd.memset(warm_in[:], 1.0)
+        nc.scalar.activation(warm_out[:], warm_in[:], ACT.Abs_reciprocal_sqrt)
         nc.sync.dma_start(lists["offs"][:], offs)
         nc.sync.dma_start(w1_raw[:].bitcast(I32), as_words(w1_words))
-        for name, source in (("two", two), ("n1", n1), ("n2", n2), ("n3", n3)):
-            nc.sync.dma_start(lists[name][:], source)
+        nc.sync.dma_start(lists["two"][:], two)
         nc.sync.dma_start(x_rows[0:P:8, :].bitcast(I32), x_scales[0].bitcast(I32))
+        for name, source in (("n1", n1), ("n2", n2), ("n3", n3)):
+            nc.sync.dma_start(lists[name][:], source)
         nc.sync.dma_start(x_table[:].bitcast(I32), as_words(x_words))
         for q in range(4):
-            nc.sync.dma_start(w1_rows[QUAD * q : QUAD * q + 4, :].bitcast(I32), w1_scales[0, 4 * q : 4 * q + 4, :].bitcast(I32))
+            queue = nc.sync if q < 3 else nc.gpsimd
+            queue.dma_start(w1_rows[QUAD * q : QUAD * q + 4, :].bitcast(I32), w1_scales[0, 4 * q : 4 * q + 4, :].bitcast(I32))
 
         gain = keep.tile([P, PACK], F32)
         rate = keep.tile([P, PACK], F32)
         nc.gpsimd.dma_start(gain[:], gn.rearrange("(p t) o -> p (t o)", t=PACK))
         nc.gpsimd.dma_start(rate[:], tau.rearrange("(p t) o -> p (t o)", t=PACK))
-
-        minus_rate = keep.tile([P, PACK], F32)
-        nc.vector.tensor_scalar(minus_rate[:], rate[:], -1.0, None, ALU.mult)
 
         y_win = [keep.tile([P, Y_WINDOW], F32, name="y_win%d" % t) for t in range(PACK)]
         h_win = [keep.tile([P, H_WINDOW], F32, name="h_win%d" % t) for t in range(PACK)]
@@ -82,12 +85,12 @@ def tile_picked_hmixharmelg_none_po_kernel(
         def pick_scales(name, tag):
             picked = keep.tile([P, S], U8, align_bytes=64, name="picked_" + name, tag=tag)
             plane = keep.tile([P, S], U8, align_bytes=64, name="plane_" + name)
+            nc.vector.memset(plane[:].bitcast(I32), 0)
             nc.vector.tensor_copy(out=picked[:], in_=x_rows[:].indirect(lists[name][:]))
-            nc.vector.tensor_copy(out=plane[:].bitcast(I32), in_=picked[:].bitcast(I32))
             return picked, plane
 
         def place_rows(queue, picked, plane):
-            for r in range(1, 4):
+            for r in range(4):
                 queue.dma_start(plane[r:P:QUAD, :].bitcast(I32), picked[8 * r : P : QUAD, :].bitcast(I32))
 
         w1_codes = keep.tile([P, H], U32, align_bytes=64)
@@ -218,10 +221,7 @@ def tile_picked_hmixharmelg_none_po_kernel(
         for t in range(PACK):
             one = slice(t, t + 1)
             nc.vector.tensor_scalar(h_win[t][:, :S], h_bank[t][:], 1.0, None, ALU.mult, ALU.max, accum_out=top[:, one])
-            if t == 0:
-                nc.scalar.activation(shift[:, one], top[:, one], ACT.Copy, scale=minus_rate[:, one])
-            else:
-                nc.vector.tensor_scalar(shift[:, one], top[:, one], minus_rate[:, one], None, ALU.mult)
+            nc.vector.tensor_scalar(shift[:, one], top[:, one], rate[:, one], -1.0, ALU.mult, ALU.mult)
         for t in range(PACK):
             one = slice(t, t + 1)
             nc.scalar.activation(ea[:, t, :], h_win[t][:].indirect(lists["n2"][:]), ACT.Exp, bias=shift[:, one], scale=rate[:, one])

@@ -21,7 +21,7 @@ QUAD = 32
 Y_WINDOW = S + 8
 H_WINDOW = 2 * S
 HALF = S // 2
-CAST_SPLIT = 192
+CAST_SPLIT = 176
 
 
 def as_words(packed):
@@ -146,20 +146,15 @@ def tile_picked_hmixharmelg_none_po_kernel(
         def square_partner(t):
             nc.scalar.activation(p_sq[:, t, :], partner[:, t, :], ACT.Square)
 
-        def add_squares(t):
-            nc.vector.tensor_tensor(both_sq[:, t, :], y_sq[:, t, :], p_sq[:, t, :], ALU.add)
-
         def numerator(t):
             nc.vector.scalar_tensor_tensor(cross[:, t, :], y_bank[t][:], gain[:, t : t + 1], partner[:, t, :], ALU.mult, ALU.mult)
 
-        def inverse_root(t):
-            nc.scalar.activation(root[:, t, :], both_sq[:, t, :], ACT.Abs_reciprocal_sqrt, bias=0.25, scale=0.5)
+        halves = [slice(0, HALF), slice(HALF, S)]
+        early = [(slice(t, t + 1), slice(0, S)) for t in range(2)]
+        late = [(slice(2, PACK), cols) for cols in halves]
 
-        def square_root_back(t):
-            if t < PACK - 1:
-                nc.vector.tensor_tensor(inverse[:, t, :], root[:, t, :], root[:, t, :], ALU.mult)
-            else:
-                nc.scalar.activation(inverse[:, t, :], root[:, t, :], ACT.Square)
+        def add_squares(ts, cols):
+            nc.vector.tensor_tensor(both_sq[:, ts, cols], y_sq[:, ts, cols], p_sq[:, ts, cols], ALU.add)
 
         for t in range(PACK):
             nc.vector.tensor_copy(out=y_win[t][:, :S], in_=y_bank[t][:])
@@ -172,11 +167,16 @@ def tile_picked_hmixharmelg_none_po_kernel(
             square_y(t)
         for t in range(PACK):
             numerator(t)
-            add_squares(t)
-        for t in range(PACK):
-            inverse_root(t)
-        for t in range(PACK):
-            square_root_back(t)
+            if t < 2:
+                add_squares(*early[t])
+        for piece in late:
+            add_squares(*piece)
+        for ts, cols in early + late:
+            nc.scalar.activation(root[:, ts, cols], both_sq[:, ts, cols], ACT.Abs_reciprocal_sqrt, bias=0.25, scale=0.5)
+        for ts, cols in early:
+            nc.vector.tensor_tensor(inverse[:, ts, cols], root[:, ts, cols], root[:, ts, cols], ALU.mult)
+        for ts, cols in late:
+            nc.scalar.activation(inverse[:, ts, cols], root[:, ts, cols], ACT.Square)
 
         deal(nc.gpsimd.tensor_copy, w3_codes[:], w23_raw[:, 0, :], 4)
         deal(nc.gpsimd.tensor_copy, w2_codes[:], w23_raw[:, 1, :], 4)
@@ -191,7 +191,6 @@ def tile_picked_hmixharmelg_none_po_kernel(
         z_rounded = keep.tile([P, S, PACK], BF16, align_bytes=64)
         z_codes = keep.tile([P, S], U32, align_bytes=64)
         z_plane = keep.tile([P, S], U8, align_bytes=64)
-        halves = [slice(0, HALF), slice(HALF, S)]
         for cols in halves:
             nc.vector.tensor_tensor(
                 z_rounded[:, cols, :].rearrange("p (c i) t -> p c t i", i=4),
@@ -214,10 +213,9 @@ def tile_picked_hmixharmelg_none_po_kernel(
         top = keep.tile([P, PACK], F32)
         shift = keep.tile([P, PACK], F32)
         ea = keep.tile([P, PACK, S], F32)
-        eb = keep.tile([P, PACK, S], F32)
+        eb = keep.tile([P, PACK, S], F32, tag="eb_then_result")
         total = keep.tile([P, PACK, S], F32)
         logs = keep.tile([P, PACK, S], F32)
-        result = keep.tile([P, PACK, S], F32)
         for t in range(PACK):
             one = slice(t, t + 1)
             nc.vector.tensor_scalar(h_win[t][:, :S], h_bank[t][:], 1.0, None, ALU.mult, ALU.max, accum_out=top[:, one])
@@ -227,6 +225,7 @@ def tile_picked_hmixharmelg_none_po_kernel(
             nc.scalar.activation(ea[:, t, :], h_win[t][:].indirect(lists["n2"][:]), ACT.Exp, bias=shift[:, one], scale=rate[:, one])
             nc.scalar.activation(eb[:, t, :], h_win[t][:].indirect(lists["n3"][:]), ACT.Exp, bias=shift[:, one], scale=rate[:, one])
             nc.vector.tensor_tensor(total[:, t, :], ea[:, t, :], eb[:, t, :], ALU.add)
+        result = keep.tile([P, PACK, S], F32, tag="eb_then_result")
         out_rows = out_0.rearrange("(p t) c -> p t c", t=PACK)
         for t in range(PACK):
             nc.scalar.activation(logs[:, t, :], total[:, t, :], ACT.Ln, bias=0.25)

@@ -18,9 +18,16 @@ ACT = mybir.ActivationFunctionType
 P = 128
 PACK = 4
 QUAD = 32
+QUADS = P // QUAD
+ROWS = 4
+GROUP = 16
+ROW_STEP = P // 16
+W2_OFFSET = 4
+LINE_WORDS, LINE_BYTES = 4, 16
 Y_WINDOW = S + 8
 H_WINDOW = 2 * S
 HALF = S // 2
+WHOLE_TILES = 2
 CAST_SPLIT = 176
 
 
@@ -35,6 +42,14 @@ def deal(engine_copy, dealt, raw, run):
     )
 
 
+def by_tiles(values):
+    return values.rearrange("p t (c i) -> p c t i", i=LINE_WORDS)
+
+
+def side_by_side(rounded):
+    return rounded.rearrange("p (c i) t -> p c t i", i=LINE_WORDS)
+
+
 def tile_picked_hmixharmelg_none_po_kernel(
     tc, x_words, x_scales, w1_words, w1_scales, gn, w2_words, w2_scales, w3_words, w3_scales, tau, offs, n1, two, n2, n3, out_0, out_1, out_2
 ):
@@ -45,7 +60,7 @@ def tile_picked_hmixharmelg_none_po_kernel(
 
         lists = {}
         for name in ("offs", "two", "n1", "n2", "n3"):
-            lists[name] = keep.tile([P, S // 16], U16, name="list_" + name)
+            lists[name] = keep.tile([P, S // GROUP], U16, name="list_" + name)
 
         x_table = keep.tile([P, T], U32, align_bytes=64)
         x_rows = keep.tile([P, T], U8, align_bytes=64, tag="rows_then_w23")
@@ -62,13 +77,13 @@ def tile_picked_hmixharmelg_none_po_kernel(
         nc.sync.dma_start(lists["offs"][:], offs)
         nc.sync.dma_start(w1_raw[:].bitcast(I32), as_words(w1_words))
         nc.sync.dma_start(lists["two"][:], two)
-        nc.sync.dma_start(x_rows[0:P:8, :].bitcast(I32), x_scales[0].bitcast(I32))
+        nc.sync.dma_start(x_rows[0:P:ROW_STEP, :].bitcast(I32), x_scales[0].bitcast(I32))
         for name, source in (("n1", n1), ("n2", n2), ("n3", n3)):
             nc.sync.dma_start(lists[name][:], source)
         nc.sync.dma_start(x_table[:].bitcast(I32), as_words(x_words))
-        for q in range(4):
-            queue = nc.sync if q < 3 else nc.gpsimd
-            queue.dma_start(w1_rows[QUAD * q : QUAD * q + 4, :].bitcast(I32), w1_scales[0, 4 * q : 4 * q + 4, :].bitcast(I32))
+        for q in range(QUADS):
+            queue = nc.sync if q < QUADS - 1 else nc.gpsimd
+            queue.dma_start(w1_rows[QUAD * q : QUAD * q + ROWS, :].bitcast(I32), w1_scales[0, ROWS * q : ROWS * (q + 1), :].bitcast(I32))
 
         gain = keep.tile([P, PACK], F32)
         rate = keep.tile([P, PACK], F32)
@@ -89,14 +104,14 @@ def tile_picked_hmixharmelg_none_po_kernel(
             nc.vector.tensor_copy(out=picked[:], in_=x_rows[:].indirect(lists[name][:]))
             return picked, plane
 
-        def place_rows(queue, picked, plane):
-            for r in range(4):
-                queue.dma_start(plane[r:P:QUAD, :].bitcast(I32), picked[8 * r : P : QUAD, :].bitcast(I32))
+        def place_rows(picked, plane):
+            for r in range(ROWS):
+                nc.sync.dma_start(plane[r:P:QUAD, :].bitcast(I32), picked[ROW_STEP * r : P : QUAD, :].bitcast(I32))
 
         w1_codes = keep.tile([P, H], U32, align_bytes=64)
-        deal(nc.scalar.copy, w1_codes[:], w1_raw[:], 4)
+        deal(nc.scalar.copy, w1_codes[:], w1_raw[:], LINE_WORDS)
         xq_picked, xq_plane = pick_scales("offs", "picked_then_w23")
-        place_rows(nc.sync, xq_picked, xq_plane)
+        place_rows(xq_picked, xq_plane)
         x2_picked, x2_plane = pick_scales("two", "picked_two")
 
         xq_codes = keep.tile([P, S], U32, align_bytes=64)
@@ -111,21 +126,22 @@ def tile_picked_hmixharmelg_none_po_kernel(
         w23_rows = keep.tile([P, N], U8, align_bytes=64, tag="picked_then_w23")
         nc.sync.dma_start(w23_raw[:, 0, :].bitcast(I32), as_words(w3_words))
         nc.sync.dma_start(w23_raw[:, 1, :].bitcast(I32), as_words(w2_words))
-        place_rows(nc.sync, x2_picked, x2_plane)
+        place_rows(x2_picked, x2_plane)
         nc.gpsimd.memset(w23_rows[:].bitcast(I32), 0)
-        for k, scales in ((0, w3_scales), (4, w2_scales)):
-            for q in range(4):
-                nc.sync.dma_start(w23_rows[QUAD * q + k : QUAD * q + k + 4, :].bitcast(I32), scales[0, 4 * q : 4 * q + 4, :].bitcast(I32))
+        for offset, scales in ((0, w3_scales), (W2_OFFSET, w2_scales)):
+            for q in range(QUADS):
+                first = QUAD * q + offset
+                nc.sync.dma_start(w23_rows[first : first + ROWS, :].bitcast(I32), scales[0, ROWS * q : ROWS * (q + 1), :].bitcast(I32))
         w3_codes = keep.tile([P, N], U32, align_bytes=64)
         w2_codes = keep.tile([P, N], U32, align_bytes=64)
         w23_plane = keep.tile([P, N], U8, align_bytes=64)
 
         y_bank = [psum.tile([P, S], F32, name="y_bank%d" % t) for t in range(PACK)]
         h_bank = [psum.tile([P, S], F32, name="h_bank%d" % t) for t in range(PACK)]
+        dealt_cols = [slice(P * t, P * (t + 1)) for t in range(PACK)]
         for t in range(PACK):
-            cols = slice(P * t, P * (t + 1))
             nc.tensor.matmul_mx(
-                out=y_bank[t][:], lhsT=w1_codes[:, cols].bitcast(FP8X4), lhsT_scale=w1_plane[:, cols],
+                out=y_bank[t][:], lhsT=w1_codes[:, dealt_cols[t]].bitcast(FP8X4), lhsT_scale=w1_plane[:, dealt_cols[t]],
                 rhs=xq_codes[:].bitcast(FP8X4), rhs_scale=xq_plane[:], start=True, stop=True,
             )
 
@@ -137,81 +153,66 @@ def tile_picked_hmixharmelg_none_po_kernel(
         root = keep.tile([P, PACK, S], F32)
         inverse = keep.tile([P, PACK, S], F32)
 
-        def fetch(t):
-            nc.scalar.activation(partner[:, t, :], y_win[t][:].indirect(lists["n1"][:]), ACT.Copy)
-
-        def square_y(t):
-            nc.vector.tensor_tensor(y_sq[:, t, :], y_bank[t][:], y_win[t][:, :S], ALU.mult)
-
         def square_partner(t):
             nc.scalar.activation(p_sq[:, t, :], partner[:, t, :], ACT.Square)
 
-        def numerator(t):
-            nc.vector.scalar_tensor_tensor(cross[:, t, :], y_bank[t][:], gain[:, t : t + 1], partner[:, t, :], ALU.mult, ALU.mult)
+        def add_squares(tiles, places):
+            nc.vector.tensor_tensor(both_sq[:, tiles, places], y_sq[:, tiles, places], p_sq[:, tiles, places], ALU.add)
 
         halves = [slice(0, HALF), slice(HALF, S)]
-        early = [(slice(t, t + 1), slice(0, S)) for t in range(2)]
-        late = [(slice(2, PACK), cols) for cols in halves]
-
-        def add_squares(ts, cols):
-            nc.vector.tensor_tensor(both_sq[:, ts, cols], y_sq[:, ts, cols], p_sq[:, ts, cols], ALU.add)
+        early = [(slice(t, t + 1), slice(0, S)) for t in range(WHOLE_TILES)]
+        late = [(slice(WHOLE_TILES, PACK), places) for places in halves]
 
         for t in range(PACK):
             nc.vector.tensor_copy(out=y_win[t][:, :S], in_=y_bank[t][:])
         for t in range(PACK):
-            fetch(t)
-            if t > 0:
+            nc.scalar.activation(partner[:, t, :], y_win[t][:].indirect(lists["n1"][:]), ACT.Copy)
+            if t > 1:
                 square_partner(t - 1)
         square_partner(PACK - 1)
         for t in range(PACK):
-            square_y(t)
+            nc.vector.tensor_tensor(y_sq[:, t, :], y_bank[t][:], y_win[t][:, :S], ALU.mult)
+        nc.vector.tensor_tensor(p_sq[:, 0, :], partner[:, 0, :], partner[:, 0, :], ALU.mult)
         for t in range(PACK):
-            numerator(t)
-            if t < 2:
+            nc.vector.scalar_tensor_tensor(cross[:, t, :], y_bank[t][:], gain[:, t : t + 1], partner[:, t, :], ALU.mult, ALU.mult)
+            if t < WHOLE_TILES:
                 add_squares(*early[t])
         for piece in late:
             add_squares(*piece)
-        for ts, cols in early + late:
-            nc.scalar.activation(root[:, ts, cols], both_sq[:, ts, cols], ACT.Abs_reciprocal_sqrt, bias=0.25, scale=0.5)
-        for ts, cols in early:
-            nc.vector.tensor_tensor(inverse[:, ts, cols], root[:, ts, cols], root[:, ts, cols], ALU.mult)
-        for ts, cols in late:
-            nc.scalar.activation(inverse[:, ts, cols], root[:, ts, cols], ACT.Square)
+        for tiles, places in early + late:
+            nc.scalar.activation(root[:, tiles, places], both_sq[:, tiles, places], ACT.Abs_reciprocal_sqrt, bias=0.25, scale=0.5)
+        for tiles, places in early:
+            nc.vector.tensor_tensor(inverse[:, tiles, places], root[:, tiles, places], root[:, tiles, places], ALU.mult)
+        for tiles, places in late:
+            nc.scalar.activation(inverse[:, tiles, places], root[:, tiles, places], ACT.Square)
 
-        deal(nc.gpsimd.tensor_copy, w3_codes[:], w23_raw[:, 0, :], 4)
-        deal(nc.gpsimd.tensor_copy, w2_codes[:], w23_raw[:, 1, :], 4)
-        deal(nc.gpsimd.tensor_copy, w23_plane[:], w23_rows[:], 16)
+        deal(nc.gpsimd.tensor_copy, w3_codes[:], w23_raw[:, 0, :], LINE_WORDS)
+        deal(nc.gpsimd.tensor_copy, w2_codes[:], w23_raw[:, 1, :], LINE_WORDS)
+        deal(nc.gpsimd.tensor_copy, w23_plane[:], w23_rows[:], LINE_BYTES)
         for t in range(PACK):
-            cols = slice(P * t, P * (t + 1))
             nc.tensor.matmul_mx(
-                out=h_bank[t][:], lhsT=w3_codes[:, cols].bitcast(FP8X4), lhsT_scale=w23_plane[:, cols],
+                out=h_bank[t][:], lhsT=w3_codes[:, dealt_cols[t]].bitcast(FP8X4), lhsT_scale=w23_plane[:, dealt_cols[t]],
                 rhs=x2_codes[:].bitcast(FP8X4), rhs_scale=x2_plane[:], start=True, stop=False,
             )
 
         z_rounded = keep.tile([P, S, PACK], BF16, align_bytes=64)
         z_codes = keep.tile([P, S], U32, align_bytes=64)
         z_plane = keep.tile([P, S], U8, align_bytes=64)
-        for cols in halves:
-            nc.vector.tensor_tensor(
-                z_rounded[:, cols, :].rearrange("p (c i) t -> p c t i", i=4),
-                cross[:, :, cols].rearrange("p t (c i) -> p c t i", i=4),
-                inverse[:, :, cols].rearrange("p t (c i) -> p c t i", i=4),
-                ALU.mult,
-            )
-        for cols in halves:
+        for places in halves:
+            nc.vector.tensor_tensor(side_by_side(z_rounded[:, places, :]), by_tiles(cross[:, :, places]), by_tiles(inverse[:, :, places]), ALU.mult)
+        for places in halves:
             nc.vector.quantize_mx(
-                out=z_codes[:, cols].bitcast(FP8X4), scales=z_plane[:, cols], in_=z_rounded[:, cols, :].rearrange("p c t -> p (c t)")
+                out=z_codes[:, places].bitcast(FP8X4), scales=z_plane[:, places], in_=z_rounded[:, places, :].rearrange("p c t -> p (c t)")
             )
         for t in range(PACK):
-            cols = slice(P * t, P * (t + 1))
             for places in halves:
                 nc.tensor.matmul_mx(
-                    out=h_bank[t][:, places], lhsT=w2_codes[:, cols].bitcast(FP8X4), lhsT_scale=w23_plane[4:P, cols],
+                    out=h_bank[t][:, places], lhsT=w2_codes[:, dealt_cols[t]].bitcast(FP8X4), lhsT_scale=w23_plane[W2_OFFSET:P, dealt_cols[t]],
                     rhs=z_codes[:, places].bitcast(FP8X4), rhs_scale=z_plane[:, places], start=False, stop=places is halves[-1],
                 )
 
         top = keep.tile([P, PACK], F32)
-        shift = keep.tile([P, PACK], F32)
+        exp_bias = keep.tile([P, PACK], F32)
         ea = keep.tile([P, PACK, S], F32)
         eb = keep.tile([P, PACK, S], F32, tag="eb_then_result")
         total = keep.tile([P, PACK, S], F32)
@@ -219,11 +220,11 @@ def tile_picked_hmixharmelg_none_po_kernel(
         for t in range(PACK):
             one = slice(t, t + 1)
             nc.vector.tensor_scalar(h_win[t][:, :S], h_bank[t][:], 1.0, None, ALU.mult, ALU.max, accum_out=top[:, one])
-            nc.vector.tensor_scalar(shift[:, one], top[:, one], rate[:, one], -1.0, ALU.mult, ALU.mult)
+            nc.vector.tensor_scalar(exp_bias[:, one], top[:, one], rate[:, one], -1.0, ALU.mult, ALU.mult)
         for t in range(PACK):
             one = slice(t, t + 1)
-            nc.scalar.activation(ea[:, t, :], h_win[t][:].indirect(lists["n2"][:]), ACT.Exp, bias=shift[:, one], scale=rate[:, one])
-            nc.scalar.activation(eb[:, t, :], h_win[t][:].indirect(lists["n3"][:]), ACT.Exp, bias=shift[:, one], scale=rate[:, one])
+            nc.scalar.activation(ea[:, t, :], h_win[t][:].indirect(lists["n2"][:]), ACT.Exp, bias=exp_bias[:, one], scale=rate[:, one])
+            nc.scalar.activation(eb[:, t, :], h_win[t][:].indirect(lists["n3"][:]), ACT.Exp, bias=exp_bias[:, one], scale=rate[:, one])
             nc.vector.tensor_tensor(total[:, t, :], ea[:, t, :], eb[:, t, :], ALU.add)
         result = keep.tile([P, PACK, S], F32, tag="eb_then_result")
         out_rows = out_0.rearrange("(p t) c -> p t c", t=PACK)
@@ -236,13 +237,10 @@ def tile_picked_hmixharmelg_none_po_kernel(
         out_rounded = keep.tile([P, S, PACK], BF16, align_bytes=64)
         out_codes = keep.tile([P, S], U32, align_bytes=64)
         out_plane = keep.tile([P, S], U8, align_bytes=64)
-        for copy, cols in ((nc.vector.tensor_copy, slice(0, CAST_SPLIT)), (nc.scalar.copy, slice(CAST_SPLIT, S))):
-            copy(
-                out=out_rounded[:, cols, :].rearrange("p (c i) t -> p c t i", i=4),
-                in_=result[:, :, cols].rearrange("p t (c i) -> p c t i", i=4),
-            )
+        for engine_copy, places in ((nc.vector.tensor_copy, slice(0, CAST_SPLIT)), (nc.scalar.copy, slice(CAST_SPLIT, S))):
+            engine_copy(out=side_by_side(out_rounded[:, places, :]), in_=by_tiles(result[:, :, places]))
         nc.vector.quantize_mx(out=out_codes[:].bitcast(FP8X4), scales=out_plane[:], in_=out_rounded[:].rearrange("p c t -> p (c t)"))
         nc.sync.dma_start(as_words(out_1), out_codes[:].bitcast(I32))
-        for q in range(4):
+        for q in range(QUADS):
             queue = nc.scalar if q % 2 else nc.sync
-            queue.dma_start(out_2[0, 4 * q : 4 * q + 4, :].bitcast(I32), out_plane[QUAD * q : QUAD * q + 4, :].bitcast(I32))
+            queue.dma_start(out_2[0, ROWS * q : ROWS * (q + 1), :].bitcast(I32), out_plane[QUAD * q : QUAD * q + ROWS, :].bitcast(I32))

from contextlib import ExitStack

import concourse.mybir as mybir

K, T, S, N, H = 512, 2048, 256, 512, 512
FLOPS = 2 * S * (K * H + H * N + K * N)

F32 = mybir.dt.float32
BF16 = mybir.dt.bfloat16
I32 = mybir.dt.int32
U32 = mybir.dt.uint32
U16 = mybir.dt.uint16
U8 = mybir.dt.uint8
FP8X4 = mybir.dt.float8_e4m3fn_x4
ALU = mybir.AluOpType
ACT = mybir.ActivationFunctionType

P = 128
PACK = 4
QUAD = 32
QUADS = P // QUAD
ROWS = 4
GROUP = 16
ROW_STEP = P // 16
W2_OFFSET = 4
LINE_WORDS, LINE_BYTES = 4, 16
Y_WINDOW = S + 8
H_WINDOW = 2 * S
HALF = S // 2
WHOLE_TILES = 2
CAST_SPLIT = 176


def as_words(packed):
    return packed[0].rearrange("p n t -> p (n t)").bitcast(I32)


def deal(engine_copy, dealt, raw, run):
    engine_copy(
        out=dealt.rearrange("p (t c i) -> p c t i", t=PACK, i=run),
        in_=raw.rearrange("p (c i t) -> p c t i", t=PACK, i=run),
    )


def by_tiles(values):
    return values.rearrange("p t (c i) -> p c t i", i=LINE_WORDS)


def side_by_side(rounded):
    return rounded.rearrange("p (c i) t -> p c t i", i=LINE_WORDS)


def tile_picked_hmixharmelg_none_po_kernel(
    tc, x_words, x_scales, w1_words, w1_scales, gn, w2_words, w2_scales, w3_words, w3_scales, tau, offs, n1, two, n2, n3, out_0, out_1, out_2
):
    nc = tc.nc
    with ExitStack() as ctx:
        keep = ctx.enter_context(tc.tile_pool(name="keep", bufs=1))
        psum = ctx.enter_context(tc.psum_pool(name="psum", bufs=1))

        lists = {}
        for name in ("offs", "two", "n1", "n2", "n3"):
            lists[name] = keep.tile([P, S // GROUP], U16, name="list_" + name)

        x_table = keep.tile([P, T], U32, align_bytes=64)
        x_rows = keep.tile([P, T], U8, align_bytes=64, tag="rows_then_w23")
        w1_raw = keep.tile([P, H], U32, align_bytes=64)
        w1_rows = keep.tile([P, H], U8, align_bytes=64)

        warm_in = keep.tile([P, 1], F32)
        warm_out = keep.tile([P, 1], F32)
        nc.vector.memset(x_rows[:, : T // 2].bitcast(I32), 0)
        nc.gpsimd.memset(x_rows[:, T // 2 :].bitcast(I32), 0)
        nc.vector.memset(w1_rows[:].bitcast(I32), 0)
        nc.gpsimd.memset(warm_in[:], 1.0)
        nc.scalar.activation(warm_out[:], warm_in[:], ACT.Abs_reciprocal_sqrt)
        nc.sync.dma_start(lists["offs"][:], offs)
        nc.sync.dma_start(w1_raw[:].bitcast(I32), as_words(w1_words))
        nc.sync.dma_start(lists["two"][:], two)
        nc.sync.dma_start(x_rows[0:P:ROW_STEP, :].bitcast(I32), x_scales[0].bitcast(I32))
        for name, source in (("n1", n1), ("n2", n2), ("n3", n3)):
            nc.sync.dma_start(lists[name][:], source)
        nc.sync.dma_start(x_table[:].bitcast(I32), as_words(x_words))
        for q in range(QUADS):
            queue = nc.sync if q < QUADS - 1 else nc.gpsimd
            queue.dma_start(w1_rows[QUAD * q : QUAD * q + ROWS, :].bitcast(I32), w1_scales[0, ROWS * q : ROWS * (q + 1), :].bitcast(I32))

        gain = keep.tile([P, PACK], F32)
        rate = keep.tile([P, PACK], F32)
        nc.gpsimd.dma_start(gain[:], gn.rearrange("(p t) o -> p (t o)", t=PACK))
        nc.gpsimd.dma_start(rate[:], tau.rearrange("(p t) o -> p (t o)", t=PACK))

        y_win = [keep.tile([P, Y_WINDOW], F32, name="y_win%d" % t) for t in range(PACK)]
        h_win = [keep.tile([P, H_WINDOW], F32, name="h_win%d" % t) for t in range(PACK)]
        for t in range(PACK):
            nc.gpsimd.memset(y_win[t][:, S:], 0.0)
        for t in range(PACK):
            nc.vector.memset(h_win[t][:, S:], 0.0)

        def pick_scales(name, tag):
            picked = keep.tile([P, S], U8, align_bytes=64, name="picked_" + name, tag=tag)
            plane = keep.tile([P, S], U8, align_bytes=64, name="plane_" + name)
            nc.vector.memset(plane[:].bitcast(I32), 0)
            nc.vector.tensor_copy(out=picked[:], in_=x_rows[:].indirect(lists[name][:]))
            return picked, plane

        def place_rows(picked, plane):
            for r in range(ROWS):
                nc.sync.dma_start(plane[r:P:QUAD, :].bitcast(I32), picked[ROW_STEP * r : P : QUAD, :].bitcast(I32))

        w1_codes = keep.tile([P, H], U32, align_bytes=64)
        deal(nc.scalar.copy, w1_codes[:], w1_raw[:], LINE_WORDS)
        xq_picked, xq_plane = pick_scales("offs", "picked_then_w23")
        place_rows(xq_picked, xq_plane)
        x2_picked, x2_plane = pick_scales("two", "picked_two")

        xq_codes = keep.tile([P, S], U32, align_bytes=64)
        x2_codes = keep.tile([P, S], U32, align_bytes=64)
        nc.vector.tensor_copy(out=xq_codes[:], in_=x_table[:].indirect(lists["offs"][:]))
        nc.vector.tensor_copy(out=x2_codes[:], in_=x_table[:].indirect(lists["two"][:]))
        w1_plane = keep.tile([P, H], U8, align_bytes=64)
        for t in range(PACK):
            nc.gpsimd.tensor_copy(out=w1_plane[:, P * t : P * (t + 1)], in_=w1_rows[:, t:H:PACK])

        w23_raw = keep.tile([P, 2, N], U32, align_bytes=64, tag="rows_then_w23")
        w23_rows = keep.tile([P, N], U8, align_bytes=64, tag="picked_then_w23")
        nc.sync.dma_start(w23_raw[:, 0, :].bitcast(I32), as_words(w3_words))
        nc.sync.dma_start(w23_raw[:, 1, :].bitcast(I32), as_words(w2_words))
        place_rows(x2_picked, x2_plane)
        nc.gpsimd.memset(w23_rows[:].bitcast(I32), 0)
        for offset, scales in ((0, w3_scales), (W2_OFFSET, w2_scales)):
            for q in range(QUADS):
                first = QUAD * q + offset
                nc.sync.dma_start(w23_rows[first : first + ROWS, :].bitcast(I32), scales[0, ROWS * q : ROWS * (q + 1), :].bitcast(I32))
        w3_codes = keep.tile([P, N], U32, align_bytes=64)
        w2_codes = keep.tile([P, N], U32, align_bytes=64)
        w23_plane = keep.tile([P, N], U8, align_bytes=64)

        y_bank = [psum.tile([P, S], F32, name="y_bank%d" % t) for t in range(PACK)]
        h_bank = [psum.tile([P, S], F32, name="h_bank%d" % t) for t in range(PACK)]
        dealt_cols = [slice(P * t, P * (t + 1)) for t in range(PACK)]
        for t in range(PACK):
            nc.tensor.matmul_mx(
                out=y_bank[t][:], lhsT=w1_codes[:, dealt_cols[t]].bitcast(FP8X4), lhsT_scale=w1_plane[:, dealt_cols[t]],
                rhs=xq_codes[:].bitcast(FP8X4), rhs_scale=xq_plane[:], start=True, stop=True,
            )

        partner = keep.tile([P, PACK, S], F32)
        y_sq = keep.tile([P, PACK, S], F32)
        p_sq = keep.tile([P, PACK, S], F32)
        both_sq = keep.tile([P, PACK, S], F32)
        cross = keep.tile([P, PACK, S], F32)
        root = keep.tile([P, PACK, S], F32)
        inverse = keep.tile([P, PACK, S], F32)

        def square_partner(t):
            nc.scalar.activation(p_sq[:, t, :], partner[:, t, :], ACT.Square)

        def add_squares(tiles, places):
            nc.vector.tensor_tensor(both_sq[:, tiles, places], y_sq[:, tiles, places], p_sq[:, tiles, places], ALU.add)

        halves = [slice(0, HALF), slice(HALF, S)]
        early = [(slice(t, t + 1), slice(0, S)) for t in range(WHOLE_TILES)]
        late = [(slice(WHOLE_TILES, PACK), places) for places in halves]

        for t in range(PACK):
            nc.vector.tensor_copy(out=y_win[t][:, :S], in_=y_bank[t][:])
        for t in range(PACK):
            nc.scalar.activation(partner[:, t, :], y_win[t][:].indirect(lists["n1"][:]), ACT.Copy)
            if t > 1:
                square_partner(t - 1)
        square_partner(PACK - 1)
        for t in range(PACK):
            nc.vector.tensor_tensor(y_sq[:, t, :], y_bank[t][:], y_win[t][:, :S], ALU.mult)
        nc.vector.tensor_tensor(p_sq[:, 0, :], partner[:, 0, :], partner[:, 0, :], ALU.mult)
        for t in range(PACK):
            nc.vector.scalar_tensor_tensor(cross[:, t, :], y_bank[t][:], gain[:, t : t + 1], partner[:, t, :], ALU.mult, ALU.mult)
            if t < WHOLE_TILES:
                add_squares(*early[t])
        for piece in late:
            add_squares(*piece)
        for tiles, places in early + late:
            nc.scalar.activation(root[:, tiles, places], both_sq[:, tiles, places], ACT.Abs_reciprocal_sqrt, bias=0.25, scale=0.5)
        for tiles, places in early:
            nc.vector.tensor_tensor(inverse[:, tiles, places], root[:, tiles, places], root[:, tiles, places], ALU.mult)
        for tiles, places in late:
            nc.scalar.activation(inverse[:, tiles, places], root[:, tiles, places], ACT.Square)

        deal(nc.gpsimd.tensor_copy, w3_codes[:], w23_raw[:, 0, :], LINE_WORDS)
        deal(nc.gpsimd.tensor_copy, w2_codes[:], w23_raw[:, 1, :], LINE_WORDS)
        deal(nc.gpsimd.tensor_copy, w23_plane[:], w23_rows[:], LINE_BYTES)
        for t in range(PACK):
            nc.tensor.matmul_mx(
                out=h_bank[t][:], lhsT=w3_codes[:, dealt_cols[t]].bitcast(FP8X4), lhsT_scale=w23_plane[:, dealt_cols[t]],
                rhs=x2_codes[:].bitcast(FP8X4), rhs_scale=x2_plane[:], start=True, stop=False,
            )

        z_rounded = keep.tile([P, S, PACK], BF16, align_bytes=64)
        z_codes = keep.tile([P, S], U32, align_bytes=64)
        z_plane = keep.tile([P, S], U8, align_bytes=64)
        for places in halves:
            nc.vector.tensor_tensor(side_by_side(z_rounded[:, places, :]), by_tiles(cross[:, :, places]), by_tiles(inverse[:, :, places]), ALU.mult)
        for places in halves:
            nc.vector.quantize_mx(
                out=z_codes[:, places].bitcast(FP8X4), scales=z_plane[:, places], in_=z_rounded[:, places, :].rearrange("p c t -> p (c t)")
            )
        for t in range(PACK):
            for places in halves:
                nc.tensor.matmul_mx(
                    out=h_bank[t][:, places], lhsT=w2_codes[:, dealt_cols[t]].bitcast(FP8X4), lhsT_scale=w23_plane[W2_OFFSET:P, dealt_cols[t]],
                    rhs=z_codes[:, places].bitcast(FP8X4), rhs_scale=z_plane[:, places], start=False, stop=places is halves[-1],
                )

        top = keep.tile([P, PACK], F32)
        exp_bias = keep.tile([P, PACK], F32)
        ea = keep.tile([P, PACK, S], F32)
        eb = keep.tile([P, PACK, S], F32, tag="eb_then_result")
        total = keep.tile([P, PACK, S], F32)
        logs = keep.tile([P, PACK, S], F32)
        for t in range(PACK):
            one = slice(t, t + 1)
            nc.vector.tensor_scalar(h_win[t][:, :S], h_bank[t][:], 1.0, None, ALU.mult, ALU.max, accum_out=top[:, one])
            nc.vector.tensor_scalar(exp_bias[:, one], top[:, one], rate[:, one], -1.0, ALU.mult, ALU.mult)
        for t in range(PACK):
            one = slice(t, t + 1)
            nc.scalar.activation(ea[:, t, :], h_win[t][:].indirect(lists["n2"][:]), ACT.Exp, bias=exp_bias[:, one], scale=rate[:, one])
            nc.scalar.activation(eb[:, t, :], h_win[t][:].indirect(lists["n3"][:]), ACT.Exp, bias=exp_bias[:, one], scale=rate[:, one])
            nc.vector.tensor_tensor(total[:, t, :], ea[:, t, :], eb[:, t, :], ALU.add)
        result = keep.tile([P, PACK, S], F32, tag="eb_then_result")
        out_rows = out_0.rearrange("(p t) c -> p t c", t=PACK)
        for t in range(PACK):
            nc.scalar.activation(logs[:, t, :], total[:, t, :], ACT.Ln, bias=0.25)
            nc.vector.tensor_tensor(result[:, t, :], h_bank[t][:], logs[:, t, :], ALU.add)
            if t % 2:
                nc.sync.dma_start(out_rows[:, t - 1 : t + 1, :], result[:, t - 1 : t + 1, :])

        out_rounded = keep.tile([P, S, PACK], BF16, align_bytes=64)
        out_codes = keep.tile([P, S], U32, align_bytes=64)
        out_plane = keep.tile([P, S], U8, align_bytes=64)
        for engine_copy, places in ((nc.vector.tensor_copy, slice(0, CAST_SPLIT)), (nc.scalar.copy, slice(CAST_SPLIT, S))):
            engine_copy(out=side_by_side(out_rounded[:, places, :]), in_=by_tiles(result[:, :, places]))
        nc.vector.quantize_mx(out=out_codes[:].bitcast(FP8X4), scales=out_plane[:], in_=out_rounded[:].rearrange("p c t -> p (c t)"))
        nc.sync.dma_start(as_words(out_1), out_codes[:].bitcast(I32))
        for q in range(QUADS):
            queue = nc.scalar if q % 2 else nc.sync
            queue.dma_start(out_2[0, ROWS * q : ROWS * (q + 1), :].bitcast(I32), out_plane[QUAD * q : QUAD * q + ROWS, :].bitcast(I32))
